import numpy as np
CORES = [21,85,149,213,277,341,405,469]
N = 8
TK = 128
D = 128 * N
EPS = 0.01
def setup_inputs(rng):
    return {"x": (rng.standard_normal((N, 128, TK), dtype=np.float32) * (0.5 + np.abs(rng.standard_normal((1, 1, TK), dtype=np.float32))) + rng.standard_normal((1, 1, TK), dtype=np.float32))}
def setup_inputs_big(rng):
    d = setup_inputs(rng)
    for k in ("x",): d[k] = (d[k].astype(np.float32) * 1024.0).astype(d[k].dtype)
    return d
def setup_inputs_small(rng):
    d = setup_inputs(rng)
    for k in ("x",): d[k] = (d[k].astype(np.float32) * (1 / 1024.0)).astype(d[k].dtype)
    return d
def setup_inputs_apart(rng):
    d = setup_inputs(rng)
    f = (10.0 ** rng.permutation(np.linspace(-1.5, 1.5, N))).astype(np.float32).reshape(N, 1, 1)
    for k in ("x",): d[k] = (d[k].astype(np.float32) * f).astype(d[k].dtype)
    return d
def setup_inputs_mixed(rng):
    d = setup_inputs(rng)
    f = (10.0 ** rng.uniform(-3, 3, (1, 1, TK))).astype(np.float32); shape = rng.integers(3, size=(1, 1, TK))
    for k in ("x",):
        x = d[k].astype(np.float32)
        m = x.mean(axis=(0, 1), keepdims=True); level = m + np.sign(x - m) * np.abs(x - m).mean(axis=(0, 1), keepdims=True) * rng.uniform(0.9, 1.1, x.shape).astype(np.float32)
        other = x * np.where(rng.random(x.shape) < 0.5, 0.1, 1.0).astype(np.float32)
        d[k] = (np.where(shape == 1, level, np.where(shape == 2, other, x)) * f).astype(d[k].dtype)
    return d
def reference(x):
    X = x.astype(np.float64)
    Z = X
    Z = Z / np.sqrt((Z ** 2).sum(axis=(0, 1)) / D + EPS)
    return {"y": Z.astype(np.float32)}

from concourse.bass import DstId, RemoteDMATransfer
from concourse.mybir import AluOpType, AxisListType, ActivationFunctionType

NS = 68
DEG = 5
POLY = [-0.622736247825211, 3.237921422967932, -7.061445266693813,
        8.35744155708686, -5.868591830565754, 2.9574103157110847]
XSCALE = 2.0 ** -22
EPS_PART = 0.01 * 2.0 ** -37
OUTSCALE = 2.0 ** -17

SCRATCH = {
    "xs": ("sbuf", [128, 128], "float32"),
    "x2": ("sbuf", [128, 128], "float32"),
    "ys": ("sbuf", [128, 128], "float32"),
    "ones": ("sbuf", [128, 128], "float32"),
    "ident": ("sbuf", [128, 128], "float32"),
    "diag": ("sbuf", [128, 128], "float32"),
    "land": ("sbuf", [128, 8], "float32"),
    "pair": ("sbuf", [128, 8], "float32"),
    "eig": ("sbuf", [128, NS + 1], "float32"),
    "two": ("sbuf", [128, NS], "float32"),
    "t3": ("sbuf", [128, NS], "float32"),
    "q": ("sbuf", [128, NS + 1], "float32"),
    "st": ("sbuf", [128, NS + 1], "float32"),
    "coef": ("sbuf", [128, DEG], "float32"),
    "ab": ("sbuf", [128, DEG], "float32"),
    "tb": ("sbuf", [128, DEG], "float32"),
    "hp": ("sbuf", [128, DEG], "float32"),
    "ps1": ("psum", [128, 4], "float32"),
    "bc": ("psum", [128, 128], "float32"),
}
SEMAPHORES = ["ld", "one", "tab", "idn", "sq", "mm", "own", "arr1", "sa", "arr2", "sab", "sv", "sbc", "sy", "stor",
              "sent"]


def _peers(c, T, topo):
    return [d for d in T.cores if d != c and topo.same_plane(c, d)]


def _partner(c, T, topo):
    return [d for d in T.cores
            if topo.rack(topo.host(d)) != topo.rack(topo.host(c)) and topo.may_write(c, d)
            and topo.chip(d) == topo.chip(c)][0]


def rank_program(g, core, T, topo):
    if T.rank_of(core) is None:
        return
    S = T.sem
    V, A, P, Y = g.vector, g.scalar, g.tensor, g.sync
    mult, add, sub, mx = AluOpType.mult, AluOpType.add, AluOpType.subtract, AluOpType.max
    n = NS

    peers = _peers(core, T, topo)
    partner = _partner(core, T, topo)
    m1 = topo.mask(core, peers[0])
    for d in peers:
        m1 &= topo.mask(core, d)
    m2 = topo.mask(core, partner)
    e1 = bin(m1).count("1")
    e2 = bin(m2).count("1")

    Y.dma_start(T.xs[:], T.x[:]).then_inc(S.ld, 16)
    V.memset(T.ones[:], 1.0).then_inc(S.one, 1)
    V.memset(T.eig[:, 0:n], 0.125).then_inc(S.tab, 1)
    V.memset(T.eig[:, n:n + 1], 2.0 ** 59).then_inc(S.tab, 1)
    V.memset(T.two[:], 2.0).then_inc(S.tab, 1)
    V.memset(T.q[:, n:n + 1], 0.0).then_inc(S.tab, 1)
    V.wait_ge(S.tab, 4)
    V.tensor_tensor_scan(T.t3[:], T.eig[:, 0:n], T.two[:], 3.0 * 2.0 ** 96, mult, mult).then_inc(S.tab, 1)
    g.wait_ge(S.one, 1)
    g.affine_select(T.ident[:], T.ones[:], [[-1, 128]], AluOpType.is_equal, 0.0, 0, 1).then_inc(S.idn, 1)

    A.wait_ge(S.ld, 16)
    A.activation(T.x2[:], T.xs[:], ActivationFunctionType.Square, scale=XSCALE).then_inc(S.sq, 1)
    P.wait_ge(S.one, 1)
    P.wait_ge(S.sq, 1)
    P.matmul(T.ps1[:, 0:1], T.x2[:], T.ones[:, 0:1], True, True).then_inc(S.mm, 1)
    V.wait_ge(S.mm, 1)
    V.tensor_scalar(T.land[:, 3:4], T.ps1[:, 0:1], EPS_PART, None, add).then_inc(S.own, 1)

    ids, dsts = [], []
    for d in peers:
        rid, pid = topo.addr(d, core)
        ids.append(DstId(rid=rid, pnc=pid))
        k = 4 + _peers(d, T, topo).index(core)
        dsts.append(T.land[:, k:k + 1])
    g.wait_ge(S.own, 1)
    g.remote_dma_fused([RemoteDMATransfer(dst_ids=ids, dma_engine_mask=m1, remote_sem=S.arr1,
                                          srcs=[T.land[:, 3:4]], dsts=dsts, alu_op=0)], local_sem=S.sent)

    for i in range(DEG):
        V.memset(T.coef[:, i:i + 1], float(POLY[i + 1] * OUTSCALE)).then_inc(S.tab, 1)

    V.wait_ge(S.own, 1)
    V.wait_ge(S.arr1, e1 * len(peers))
    V.tensor_reduce(T.pair[:, 3:4], T.land[:, 3:4 + len(peers)], AxisListType.X, add).then_inc(S.sa, 1)
    rid, pid = topo.addr(partner, core)
    g.wait_ge(S.sa, 1)
    g.remote_dma(T.pair[:, 4:5], T.pair[:, 3:4], S.arr2, S.sent, pid, rid, m2)

    A.wait_ge(S.one, 1)
    A.wait_ge(S.sa, 1)
    A.wait_ge(S.arr2, e2)
    A.activation(T.ab[:], T.ones[:, 0:DEG], ActivationFunctionType.Identity,
                 bias=T.pair[:, 3:4], scale=T.pair[:, 4:5]).then_inc(S.sab, 1)
    V.wait_ge(S.tab, 5 + DEG)
    V.wait_ge(S.sa, 1)
    V.wait_ge(S.arr2, e2)
    V.tensor_scalar(T.q[:, 0:n], T.t3[:], T.pair[:, 3:4], T.pair[:, 4:5], sub, sub).then_inc(S.sv, 1)
    V.wait_ge(S.sv, 1)
    V.tensor_tensor_scan(T.st[:], T.eig[:], T.q[:], 0.0, mult, mx).then_inc(S.sv, 1)
    V.wait_ge(S.sv, 2)
    V.wait_ge(S.sab, 1)
    V.tensor_scalar(T.tb[:], T.ab[:], T.st[:, n:n + 1], T.st[:, n:n + 1], mult, mult).then_inc(S.sv, 1)
    V.wait_ge(S.sv, 3)
    V.tensor_tensor_scan(T.hp[:], T.tb[:], T.coef[:], float(POLY[0] * OUTSCALE), mult, add).then_inc(S.sv, 1)
    V.wait_ge(S.sv, 4)
    V.wait_ge(S.idn, 1)
    V.tensor_scalar(T.diag[:], T.ident[:], T.st[:, n:n + 1], T.hp[:, DEG - 1:DEG], mult, mult).then_inc(S.sv, 1)

    P.wait_ge(S.sv, 5)
    P.matmul(T.bc[:], T.ones[:], T.diag[:], True, True).then_inc(S.sbc, 1)
    V.wait_ge(S.ld, 16)
    V.wait_ge(S.sbc, 1)
    V.tensor_tensor(T.ys[:], T.xs[:], T.bc[:], mult).then_inc(S.sy, 1)
    Y.wait_ge(S.sy, 1)
    Y.dma_start(T.y[:], T.ys[:]).then_inc(S.stor, 16)
    Y.wait_ge(S.stor, 16)
    g.wait_ge(S.sent, e1 + e2)
